import numpy as np, ml_dtypes
CORES = [8,80,112,136,208,240,264,336,368,392,464,496]
N = 12
NH, QP = 2, 128
def setup_inputs(rng):
    return {"q": rng.standard_normal((N, 128, NH * QP), dtype=np.float32).astype(ml_dtypes.bfloat16), "k": rng.standard_normal((N, 128, NH * 128), dtype=np.float32).astype(ml_dtypes.bfloat16), "v": rng.standard_normal((N, 128, NH * 128), dtype=np.float32).astype(ml_dtypes.bfloat16)}
def setup_inputs_big(rng):
    d = setup_inputs(rng)
    for k in ("q", "k", "v"): d[k] = (d[k].astype(np.float32) * 1024.0).astype(d[k].dtype)
    return d
def setup_inputs_small(rng):
    d = setup_inputs(rng)
    for k in ("q", "k", "v"): d[k] = (d[k].astype(np.float32) * (1 / 1024.0)).astype(d[k].dtype)
    return d
def setup_inputs_apart(rng):
    d = setup_inputs(rng)
    f = (10.0 ** rng.permutation(np.linspace(-1.5, 1.5, N))).astype(np.float32).reshape(N, 1, 1)
    for k in ("q", "k", "v"): d[k] = (d[k].astype(np.float32) * f).astype(d[k].dtype)
    return d
def reference(q, k, v):
    Q, K, V = q.astype(np.float64), k.astype(np.float64), v.astype(np.float64)
    y = np.zeros((N, 128, NH * QP))
    for r in range(N):
        for h in range(NH):
            for j in range(N):
                S = np.maximum(K[j][:, 128 * h:128 * h + 128].T @ Q[r][:, QP * h:QP * h + QP], 0.0)
                y[r][:, QP * h:QP * h + QP] += V[j][:, 128 * h:128 * h + 128].T @ S
    return {"y": y.astype(ml_dtypes.bfloat16 if q.dtype != np.float64 else np.float64)}

@@ -1,0 +1,236 @@
+from concourse.bass import DstId, RemoteDMATransfer
+from concourse.mybir import AluOpType
+
+NSIM = 512
+D = 128
+TILES = [(0, "a"), (1, "a"), (2, "a"), (0, "b"), (1, "b"), (2, "b"), (3, "b"), (3, "a")]
+NSB = 6
+
+SCRATCH = {
+    "own": ("sbuf", [128, 2, 3 * D], "bfloat16"),
+    "big": ("sbuf", [128, 5 * D], "bfloat16"),
+    "kvin": ("sbuf", [128, 4 * 2 * D], "bfloat16"),
+    "zeros": ("sbuf", [128, 2 * D], "float32"),
+    "ssb": ("sbuf", [128, 12 * D], "bfloat16"),
+    "osb": ("sbuf", [128, 3 * D], "bfloat16"),
+    "part": ("sbuf", [128, 3 * 2 * D], "bfloat16"),
+    "ysb": ("sbuf", [128, 2 * D], "bfloat16"),
+    "psa": ("psum", [128, 512], "float32"),
+    "psb": ("psum", [128, 512], "float32"),
+}
+for _b in range(NSB):
+    SCRATCH["ps%d" % _b] = ("psum", [128, 512], "float32")
+
+SEMAPHORES = (["ldk", "ldv", "ldq", "snd", "pt0", "pt1", "pt2", "a1", "a2", "st",
+               "own", "kvh0", "kvh1", "kvh2", "kvh3", "qin", "zs", "oa", "ob", "ca", "cb"]
+              + ["m%d" % t for t in range(len(TILES))] + ["r%d" % t for t in range(len(TILES))])
+
+_PLAN = {}
+
+
+def _bits(m):
+    return [b for b in range(m.bit_length()) if (m >> b) & 1]
+
+
+def _mk(bs):
+    return sum(1 << b for b in bs)
+
+
+def _plan(T, topo):
+    if "p" in _PLAN:
+        return _PLAN["p"]
+    cores = list(T.cores)
+    n = len(cores)
+    info, role = [], {}
+    for i, R in enumerate(cores):
+        row = [j for j in range(n) if topo.host(cores[j]) == topo.host(R)]
+        col = [j for j in range(n) if topo.chip(cores[j]) == topo.chip(R) and j != i]
+        chip = [c for c in range(NSIM) if topo.host(c) == topo.host(R) and topo.chip(c) == topo.chip(R) and c != R]
+        able = [c for c in chip if all(topo.may_write(c, cores[j]) for j in row if j != i)]
+        p0 = [c for c in able if topo.die(c) == topo.die(R)][0]
+        p1 = [c for c in able if topo.die(c) != topo.die(R)][0]
+        rm = [j for j in col if topo.rack(topo.host(cores[j])) == topo.rack(topo.host(R))][0]
+        dg = [j for j in col if not topo.may_write(R, cores[j])][0]
+        cb = [j for j in col if j not in (rm, dg)][0]
+        info.append({"R": R, "row": row, "oth": [j for j in row if j != i], "P": (p0, p1), "rm": rm, "cb": cb, "dg": dg,
+                     "host": topo.host(R), "place": row.index(i)})
+        role[R] = ("R", i, 0)
+        role[p0] = ("P", i, 0)
+        role[p1] = ("P", i, 1)
+    _PLAN["p"] = (info, role)
+    return _PLAN["p"]
+
+
+def _eng(topo, src, dst):
+    return _bits(topo.mask(src, dst))
+
+
+def _dst(topo, dst, src):
+    rid, pid = topo.addr(dst, src)
+    return DstId(rid=rid, pnc=pid)
+
+
+def _rank_core(g, core, T, topo, info, i):
+    d, S = info[i], T.sem
+    g.sync.dma_start(T.own[:, :, 2 * D:3 * D], T.q[:, :]).then_inc(S.ldq, 16)
+    g.scalar.dma_start(T.own[:, :, 0:D], T.k[:, :]).then_inc(S.ldk, 16)
+    g.sync.dma_start(T.own[:, :, D:2 * D], T.v[:, :]).then_inc(S.ldv, 16)
+    g.wait_ge(S.ldq, 16)
+    g.wait_ge(S.ldk, 16)
+    g.wait_ge(S.ldv, 16)
+    sent = 0
+    al = _eng(topo, core, d["P"][0])
+    half = len(al) // 2
+    g.remote_dma_fused([
+        RemoteDMATransfer(dst_ids=[_dst(topo, d["P"][x], core)], dma_engine_mask=_mk(al[x * half:(x + 1) * half]),
+                          remote_sem=S.own, src=T.own[:, x, :], dst=T.big[:, 0:3 * D]) for x in (0, 1)], local_sem=S.snd)
+    sent += 2 * half
+    slot = T.kvin[:, 2 * D * d["host"]:2 * D * (d["host"] + 1)]
+    for pair in ((d["rm"], d["cb"]), (d["cb"], d["rm"])):
+        tr = []
+        for x in (0, 1):
+            to = info[pair[x]]["P"][x]
+            lo = _eng(topo, core, to)
+            hl = len(lo) // 2
+            tr.append(RemoteDMATransfer(dst_ids=[_dst(topo, to, core)], dma_engine_mask=_mk(lo[x * hl:(x + 1) * hl]),
+                                        remote_sem=S["kvh%d" % d["host"]], src=T.own[:, x, 0:2 * D], dst=slot))
+            sent += hl
+        g.remote_dma_fused(tr, local_sem=S.snd)
+    oth = sorted(d["oth"], key=lambda j: 0 if topo.same_plane(core, info[j]["R"]) else 1)
+
+    def got(j):
+        return sum(len(_eng(topo, info[j]["P"][x], core)) // (1 if j == i else 2) // (2 if j == i else 1) for x in (0, 1))
+
+    def blk(j):
+        p = info[j]["place"]
+        return T.part[:, 2 * D * p:2 * D * (p + 1)]
+
+    v = g.vector
+    v.wait_ge(S["pt%d" % d["place"]], got(i))
+    v.wait_ge(S["pt%d" % info[oth[0]]["place"]], got(oth[0]))
+    v.tensor_tensor(T.ps0[:, 0:2 * D], blk(i), blk(oth[0]), AluOpType.add).then_inc(S.a1, 1)
+    v.wait_ge(S.a1, 1)
+    v.wait_ge(S["pt%d" % info[oth[1]]["place"]], got(oth[1]))
+    v.tensor_tensor(T.ysb[:, :], T.ps0[:, 0:2 * D], blk(oth[1]), AluOpType.add).then_inc(S.a2, 1)
+    g.sync.wait_ge(S.a2, 1)
+    g.sync.dma_start(T.y[:, :], T.ysb[:, :]).then_inc(S.st, 16)
+    g.sync.wait_ge(S.st, 16)
+    g.wait_ge(S.snd, sent)
+
+
+def _compute_core(g, core, T, topo, info, i, x):
+    d, S = info[i], T.sem
+    R = d["R"]
+    first, second = (d["rm"], d["cb"]) if x == 0 else (d["cb"], d["rm"])
+    onward = second
+    n_own = len(_eng(topo, R, core)) // 2
+
+    def kv_sem(j):
+        return S["kvh%d" % info[j]["host"]]
+
+    def kv_cols(j):
+        return 2 * D * info[j]["host"]
+
+    n_dir = {j: len(_eng(topo, info[j]["R"], core)) // 2 for j in (first, second)}
+    n_fwd = len(_eng(topo, info[second]["P"][x], core))
+    n_q = sum(len(_eng(topo, info[j]["P"][x], core)) for j in d["oth"])
+
+    sent = 0
+    g.wait_ge(S.own, n_own)
+    lo = _eng(topo, core, info[d["oth"][0]]["P"][x])
+    dsts = []
+    for j in d["oth"]:
+        s = 1 + info[j]["oth"].index(i)
+        dsts.append(T.big[:, (2 + s) * D:(3 + s) * D])
+    g.remote_dma_fused([RemoteDMATransfer(dst_ids=[_dst(topo, info[j]["P"][x], core) for j in d["oth"]],
+                                          dma_engine_mask=_mk(lo), remote_sem=S.qin,
+                                          srcs=[T.big[:, 2 * D:3 * D]], dsts=dsts)], local_sem=S.snd)
+    sent += len(lo)
+    g.wait_ge(kv_sem(first), n_dir[first])
+    to = info[onward]["P"][x]
+    rid, pid = topo.addr(to, core)
+    lo = _eng(topo, core, to)
+    ap = T.kvin[:, kv_cols(first):kv_cols(first) + 2 * D]
+    g.remote_dma(ap, ap, kv_sem(first), S.snd, pid, rid, _mk(lo))
+    sent += len(lo)
+    g.wait_ge(S.cb, 1)
+    here = (2 * d["place"] + x) * D
+    tr = []
+    for k, j in enumerate(d["oth"]):
+        lo = _eng(topo, core, info[j]["R"])
+        hl = len(lo) // 2
+        tr.append(RemoteDMATransfer(dst_ids=[_dst(topo, info[j]["R"], core)], dma_engine_mask=_mk(lo[k * hl:(k + 1) * hl]),
+                                    remote_sem=S["pt%d" % d["place"]], src=T.osb[:, (1 + k) * D:(2 + k) * D],
+                                    dst=T.part[:, here:here + D]))
+        sent += hl
+    g.remote_dma_fused(tr, local_sem=S.snd)
+    g.wait_ge(S.ca, 1)
+    off = _eng(topo, core, info[d["oth"][0]]["R"])
+    hi = [b for b in _eng(topo, core, R) if b not in off]
+    rid, pid = topo.addr(R, core)
+    g.remote_dma(T.part[:, here:here + D], T.osb[:, 0:D], S["pt%d" % d["place"]], S.snd, pid, rid, _mk(hi))
+    sent += len(hi)
+    g.wait_ge(S.snd, sent)
+
+    K = [T.big[:, 0:D]] + [T.kvin[:, kv_cols(j):kv_cols(j) + D] for j in (first, second, d["dg"])]
+    V = [T.big[:, D:2 * D]] + [T.kvin[:, kv_cols(j) + D:kv_cols(j) + 2 * D] for j in (first, second, d["dg"])]
+    Q = {"a": T.big[:, 2 * D:3 * D], "b": T.big[:, 3 * D:5 * D]}
+    W = {"a": D, "b": 2 * D}
+    ACC = {"a": T.psa[:, 0:D], "b": T.psb[:, 0:2 * D]}
+    DONE = {"a": S.oa, "b": S.ob}
+    offs, o = [], 0
+    for (_, grp) in TILES:
+        offs.append(o)
+        o += W[grp]
+    arrive = [(S.own, n_own), (kv_sem(first), n_dir[first]), (kv_sem(second), n_dir[second]), (kv_sem(d["dg"]), n_fwd)]
+
+    te = g.tensor
+    seen = {"k": set(), "q": False}
+
+    def s_mm(t):
+        j, grp = TILES[t]
+        if j not in seen["k"]:
+            te.wait_ge(arrive[j][0], arrive[j][1])
+            seen["k"].add(j)
+        if grp == "b" and not seen["q"]:
+            te.wait_ge(S.qin, n_q)
+            seen["q"] = True
+        te.matmul(T["ps%d" % (t % NSB)][:, 0:W[grp]], K[j], Q[grp], True, True).then_inc(S["m%d" % t], 1)
+
+    def o_mm(t):
+        j, grp = TILES[t]
+        same = [u for u in range(len(TILES)) if TILES[u][1] == grp]
+        te.wait_ge(S["r%d" % t], 1)
+        mm = te.matmul(ACC[grp], V[j], T.ssb[:, offs[t]:offs[t] + W[grp]], t == same[0], t == same[-1])
+        if t == same[-1]:
+            mm.then_inc(DONE[grp], 1)
+
+    for kind, t in (("s", 0), ("s", 1), ("o", 0), ("s", 2), ("o", 1), ("s", 3), ("o", 2), ("s", 4), ("o", 3), ("s", 5),
+                    ("o", 4), ("o", 5), ("s", 6), ("s", 7), ("o", 6), ("o", 7)):
+        if kind == "s":
+            s_mm(t)
+        else:
+            o_mm(t)
+
+    v = g.vector
+    v.memset(T.zeros[:, :], 0.0).then_inc(S.zs, 1)
+    v.wait_ge(S.zs, 1)
+    for t, (_, grp) in enumerate(TILES):
+        v.wait_ge(S["m%d" % t], 1)
+        v.tensor_tensor(T.ssb[:, offs[t]:offs[t] + W[grp]], T["ps%d" % (t % NSB)][:, 0:W[grp]], T.zeros[:, 0:W[grp]],
+                        AluOpType.max).then_inc(S["r%d" % t], 1)
+    v.wait_ge(S.ob, 1)
+    v.tensor_copy(T.osb[:, D:3 * D], T.psb[:, 0:2 * D]).then_inc(S.cb, 1)
+    v.wait_ge(S.oa, 1)
+    v.tensor_copy(T.osb[:, 0:D], T.psa[:, 0:D]).then_inc(S.ca, 1)
+
+
+def rank_program(g, core, T, topo):
+    info, role = _plan(T, topo)
+    if core not in role:
+        return
+    kind, i, x = role[core]
+    if kind == "R":
+        _rank_core(g, core, T, topo, info, i)
+    else:
+        _compute_core(g, core, T, topo, info, i, x)

@@ -3,12 +3,13 @@ from concourse.mybir import AluOpType
 
 NSIM = 512
 D = 128
-TILES = [(0, "a"), (1, "a"), (2, "a"), (0, "b"), (1, "b"), (2, "b"), (3, "b"), (3, "a")]
+TILES = [(1, "a"), (1, "b"), (0, "a"), (0, "b"), (2, "a"), (2, "b"), (3, "a"), (3, "b")]
 NSB = 6
 
 SCRATCH = {
-    "own": ("sbuf", [128, 2, 3 * D], "bfloat16"),
-    "big": ("sbuf", [128, 5 * D], "bfloat16"),
+    "qsb": ("sbuf", [128, 2 * D], "bfloat16"),
+    "kv": ("sbuf", [128, 4 * D], "bfloat16"),
+    "big": ("sbuf", [128, 3 * D], "bfloat16"),
     "kvin": ("sbuf", [128, 4 * 2 * D], "bfloat16"),
     "zeros": ("sbuf", [128, 2 * D], "float32"),
     "ssb": ("sbuf", [128, 12 * D], "bfloat16"),
@@ -21,7 +22,7 @@ SCRATCH = {
 for _b in range(NSB):
     SCRATCH["ps%d" % _b] = ("psum", [128, 512], "float32")
 
-SEMAPHORES = (["ldk", "ldv", "ldq", "snd", "pt0", "pt1", "pt2", "a1", "a2", "st",
+SEMAPHORES = (["ldk", "ldv0", "ldv1", "ldq", "snd", "pt0", "pt1", "pt2", "a0", "a1", "a2", "st",
                "own", "kvh0", "kvh1", "kvh2", "kvh3", "qin", "zs", "oa", "ob", "ca", "cb"]
               + ["m%d" % t for t in range(len(TILES))] + ["r%d" % t for t in range(len(TILES))])
 
@@ -72,34 +73,44 @@ def _dst(topo, dst, src):
 
 def _rank_core(g, core, T, topo, info, i):
     d, S = info[i], T.sem
-    g.sync.dma_start(T.own[:, :, 2 * D:3 * D], T.q[:, :]).then_inc(S.ldq, 16)
-    g.scalar.dma_start(T.own[:, :, 0:D], T.k[:, :]).then_inc(S.ldk, 16)
-    g.sync.dma_start(T.own[:, :, D:2 * D], T.v[:, :]).then_inc(S.ldv, 16)
-    g.wait_ge(S.ldq, 16)
-    g.wait_ge(S.ldk, 16)
-    g.wait_ge(S.ldv, 16)
-    sent = 0
     al = _eng(topo, core, d["P"][0])
-    half = len(al) // 2
+    lo = _eng(topo, core, info[d["rm"]]["P"][0])
+    hi = [b for b in al if b not in lo]
+    g.sync.dma_start(T.qsb[:, :], T.q[:, :]).then_inc(S.ldq, 16)
+    g.scalar.dma_start(T.kv[:, D:3 * D], T.k[:, :]).then_inc(S.ldk, 16)
+    g.sync.dma_start(T.kv[:, 0:D], T.v[:, 0:D]).then_inc(S.ldv0, 16)
+    g.scalar.dma_start(T.kv[:, 3 * D:4 * D], T.v[:, D:2 * D]).then_inc(S.ldv1, 16)
+    sent = 0
+    g.wait_ge(S.ldq, 16)
     g.remote_dma_fused([
-        RemoteDMATransfer(dst_ids=[_dst(topo, d["P"][x], core)], dma_engine_mask=_mk(al[x * half:(x + 1) * half]),
-                          remote_sem=S.own, src=T.own[:, x, :], dst=T.big[:, 0:3 * D]) for x in (0, 1)], local_sem=S.snd)
-    sent += 2 * half
+        RemoteDMATransfer(dst_ids=[_dst(topo, d["P"][x], core)], dma_engine_mask=_mk(hi[x::2]),
+                          remote_sem=S.own, src=T.qsb[:, x * D:(x + 1) * D], dst=T.big[:, 0:D]) for x in (0, 1)],
+        local_sem=S.snd)
+    sent += len(hi)
+    g.wait_ge(S.ldk, 16)
+    g.wait_ge(S.ldv0, 16)
+    g.wait_ge(S.ldv1, 16)
     slot = T.kvin[:, 2 * D * d["host"]:2 * D * (d["host"] + 1)]
-    for pair in ((d["rm"], d["cb"]), (d["cb"], d["rm"])):
+    for n, pair in enumerate(((d["rm"], d["cb"]), (d["cb"], d["rm"]))):
         tr = []
         for x in (0, 1):
             to = info[pair[x]]["P"][x]
-            lo = _eng(topo, core, to)
-            hl = len(lo) // 2
-            tr.append(RemoteDMATransfer(dst_ids=[_dst(topo, to, core)], dma_engine_mask=_mk(lo[x * hl:(x + 1) * hl]),
-                                        remote_sem=S["kvh%d" % d["host"]], src=T.own[:, x, 0:2 * D], dst=slot))
-            sent += hl
+            par = 0 if pair[x] == d["rm"] else 1
+            tr.append(RemoteDMATransfer(dst_ids=[_dst(topo, to, core)], dma_engine_mask=_mk(lo[par::2]),
+                                        remote_sem=S["kvh%d" % d["host"]], src=T.kv[:, 2 * D * x:2 * D * (x + 1)], dst=slot))
+            sent += len(lo[par::2])
+            if n == 1:
+                tr.append(RemoteDMATransfer(dst_ids=[_dst(topo, d["P"][x], core)], dma_engine_mask=_mk(hi[x::2]),
+                                            remote_sem=S["kvh%d" % d["host"]], src=T.kv[:, 2 * D * x:2 * D * (x + 1)],
+                                            dst=slot))
+                sent += len(hi[x::2])
         g.remote_dma_fused(tr, local_sem=S.snd)
     oth = sorted(d["oth"], key=lambda j: 0 if topo.same_plane(core, info[j]["R"]) else 1)
 
     def got(j):
-        return sum(len(_eng(topo, info[j]["P"][x], core)) // (1 if j == i else 2) // (2 if j == i else 1) for x in (0, 1))
+        if j == i:
+            return sum(len(_eng(topo, d["P"][x], info[d["oth"][0]]["R"])) for x in (0, 1))
+        return sum(len(_eng(topo, info[j]["P"][x], core)) // 2 for x in (0, 1))
 
     def blk(j):
         p = info[j]["place"]
@@ -107,11 +118,13 @@ def _rank_core(g, core, T, topo, info, i):
 
     v = g.vector
     v.wait_ge(S["pt%d" % d["place"]], got(i))
+    v.tensor_copy(T.ps0[:, 0:2 * D], blk(i)).then_inc(S.a0, 1)
+    v.wait_ge(S.a0, 1)
     v.wait_ge(S["pt%d" % info[oth[0]]["place"]], got(oth[0]))
-    v.tensor_tensor(T.ps0[:, 0:2 * D], blk(i), blk(oth[0]), AluOpType.add).then_inc(S.a1, 1)
+    v.tensor_tensor(T.ps1[:, 0:2 * D], T.ps0[:, 0:2 * D], blk(oth[0]), AluOpType.add).then_inc(S.a1, 1)
     v.wait_ge(S.a1, 1)
     v.wait_ge(S["pt%d" % info[oth[1]]["place"]], got(oth[1]))
-    v.tensor_tensor(T.ysb[:, :], T.ps0[:, 0:2 * D], blk(oth[1]), AluOpType.add).then_inc(S.a2, 1)
+    v.tensor_tensor(T.ysb[:, :], T.ps1[:, 0:2 * D], blk(oth[1]), AluOpType.add).then_inc(S.a2, 1)
     g.sync.wait_ge(S.a2, 1)
     g.sync.dma_start(T.y[:, :], T.ysb[:, :]).then_inc(S.st, 16)
     g.sync.wait_ge(S.st, 16)
@@ -123,7 +136,8 @@ def _compute_core(g, core, T, topo, info, i, x):
     R = d["R"]
     first, second = (d["rm"], d["cb"]) if x == 0 else (d["cb"], d["rm"])
     onward = second
-    n_own = len(_eng(topo, R, core)) // 2
+    off_r = _eng(topo, R, info[first]["P"][x])
+    n_own = (len(_eng(topo, R, core)) - len(off_r)) // 2
 
     def kv_sem(j):
         return S["kvh%d" % info[j]["host"]]
@@ -141,10 +155,10 @@ def _compute_core(g, core, T, topo, info, i, x):
     dsts = []
     for j in d["oth"]:
         s = 1 + info[j]["oth"].index(i)
-        dsts.append(T.big[:, (2 + s) * D:(3 + s) * D])
+        dsts.append(T.big[:, s * D:(1 + s) * D])
     g.remote_dma_fused([RemoteDMATransfer(dst_ids=[_dst(topo, info[j]["P"][x], core) for j in d["oth"]],
                                           dma_engine_mask=_mk(lo), remote_sem=S.qin,
-                                          srcs=[T.big[:, 2 * D:3 * D]], dsts=dsts)], local_sem=S.snd)
+                                          srcs=[T.big[:, 0:D]], dsts=dsts)], local_sem=S.snd)
     sent += len(lo)
     g.wait_ge(kv_sem(first), n_dir[first])
     to = info[onward]["P"][x]
@@ -153,8 +167,13 @@ def _compute_core(g, core, T, topo, info, i, x):
     ap = T.kvin[:, kv_cols(first):kv_cols(first) + 2 * D]
     g.remote_dma(ap, ap, kv_sem(first), S.snd, pid, rid, _mk(lo))
     sent += len(lo)
-    g.wait_ge(S.cb, 1)
     here = (2 * d["place"] + x) * D
+    g.wait_ge(S.ca, 1)
+    off = _eng(topo, core, info[d["oth"][0]]["R"])
+    rid, pid = topo.addr(R, core)
+    g.remote_dma(T.part[:, here:here + D], T.osb[:, 0:D], S["pt%d" % d["place"]], S.snd, pid, rid, _mk(off))
+    sent += len(off)
+    g.wait_ge(S.cb, 1)
     tr = []
     for k, j in enumerate(d["oth"]):
         lo = _eng(topo, core, info[j]["R"])
@@ -164,17 +183,13 @@ def _compute_core(g, core, T, topo, info, i, x):
                                     dst=T.part[:, here:here + D]))
         sent += hl
     g.remote_dma_fused(tr, local_sem=S.snd)
-    g.wait_ge(S.ca, 1)
-    off = _eng(topo, core, info[d["oth"][0]]["R"])
-    hi = [b for b in _eng(topo, core, R) if b not in off]
-    rid, pid = topo.addr(R, core)
-    g.remote_dma(T.part[:, here:here + D], T.osb[:, 0:D], S["pt%d" % d["place"]], S.snd, pid, rid, _mk(hi))
-    sent += len(hi)
     g.wait_ge(S.snd, sent)
 
-    K = [T.big[:, 0:D]] + [T.kvin[:, kv_cols(j):kv_cols(j) + D] for j in (first, second, d["dg"])]
-    V = [T.big[:, D:2 * D]] + [T.kvin[:, kv_cols(j) + D:kv_cols(j) + 2 * D] for j in (first, second, d["dg"])]
-    Q = {"a": T.big[:, 2 * D:3 * D], "b": T.big[:, 3 * D:5 * D]}
+    ko, vo = (D, 0) if x == 0 else (0, D)
+    blocks = (i, first, second, d["dg"])
+    K = [T.kvin[:, kv_cols(j) + ko:kv_cols(j) + ko + D] for j in blocks]
+    V = [T.kvin[:, kv_cols(j) + vo:kv_cols(j) + vo + D] for j in blocks]
+    Q = {"a": T.big[:, 0:D], "b": T.big[:, D:3 * D]}
     W = {"a": D, "b": 2 * D}
     ACC = {"a": T.psa[:, 0:D], "b": T.psb[:, 0:2 * D]}
     DONE = {"a": S.oa, "b": S.ob}
@@ -182,13 +197,16 @@ def _compute_core(g, core, T, topo, info, i, x):
     for (_, grp) in TILES:
         offs.append(o)
         o += W[grp]
-    arrive = [(S.own, n_own), (kv_sem(first), n_dir[first]), (kv_sem(second), n_dir[second]), (kv_sem(d["dg"]), n_fwd)]
+    arrive = [(kv_sem(i), n_own), (kv_sem(first), n_dir[first]), (kv_sem(second), n_dir[second]), (kv_sem(d["dg"]), n_fwd)]
 
     te = g.tensor
-    seen = {"k": set(), "q": False}
+    seen = {"k": set(), "q": False, "o": False}
 
     def s_mm(t):
         j, grp = TILES[t]
+        if not seen["o"]:
+            te.wait_ge(S.own, n_own)
+            seen["o"] = True
         if j not in seen["k"]:
             te.wait_ge(arrive[j][0], arrive[j][1])
             seen["k"].add(j)
@@ -219,10 +237,10 @@ def _compute_core(g, core, T, topo, info, i, x):
         v.wait_ge(S["m%d" % t], 1)
         v.tensor_tensor(T.ssb[:, offs[t]:offs[t] + W[grp]], T["ps%d" % (t % NSB)][:, 0:W[grp]], T.zeros[:, 0:W[grp]],
                         AluOpType.max).then_inc(S["r%d" % t], 1)
-    v.wait_ge(S.ob, 1)
-    v.tensor_copy(T.osb[:, D:3 * D], T.psb[:, 0:2 * D]).then_inc(S.cb, 1)
     v.wait_ge(S.oa, 1)
     v.tensor_copy(T.osb[:, 0:D], T.psa[:, 0:D]).then_inc(S.ca, 1)
+    v.wait_ge(S.ob, 1)
+    v.tensor_copy(T.osb[:, D:3 * D], T.psb[:, 0:2 * D]).then_inc(S.cb, 1)
 
 
 def rank_program(g, core, T, topo):

from concourse.bass import DstId, RemoteDMATransfer
from concourse.mybir import AluOpType

NSIM = 512
D = 128
TILES = [(1, "a"), (1, "b"), (0, "a"), (0, "b"), (2, "a"), (2, "b"), (3, "a"), (3, "b")]
NSB = 6

SCRATCH = {
    "qsb": ("sbuf", [128, 2 * D], "bfloat16"),
    "kv": ("sbuf", [128, 4 * D], "bfloat16"),
    "big": ("sbuf", [128, 3 * D], "bfloat16"),
    "kvin": ("sbuf", [128, 4 * 2 * D], "bfloat16"),
    "zeros": ("sbuf", [128, 2 * D], "float32"),
    "ssb": ("sbuf", [128, 12 * D], "bfloat16"),
    "osb": ("sbuf", [128, 3 * D], "bfloat16"),
    "part": ("sbuf", [128, 3 * 2 * D], "bfloat16"),
    "ysb": ("sbuf", [128, 2 * D], "bfloat16"),
    "psa": ("psum", [128, 512], "float32"),
    "psb": ("psum", [128, 512], "float32"),
}
for _b in range(NSB):
    SCRATCH["ps%d" % _b] = ("psum", [128, 512], "float32")

SEMAPHORES = (["ldk", "ldv0", "ldv1", "ldq", "snd", "pt0", "pt1", "pt2", "a0", "a1", "a2", "st",
               "own", "kvh0", "kvh1", "kvh2", "kvh3", "qin", "zs", "oa", "ob", "ca", "cb"]
              + ["m%d" % t for t in range(len(TILES))] + ["r%d" % t for t in range(len(TILES))])

_PLAN = {}


def _bits(m):
    return [b for b in range(m.bit_length()) if (m >> b) & 1]


def _mk(bs):
    return sum(1 << b for b in bs)


def _plan(T, topo):
    if "p" in _PLAN:
        return _PLAN["p"]
    cores = list(T.cores)
    n = len(cores)
    info, role = [], {}
    for i, R in enumerate(cores):
        row = [j for j in range(n) if topo.host(cores[j]) == topo.host(R)]
        col = [j for j in range(n) if topo.chip(cores[j]) == topo.chip(R) and j != i]
        chip = [c for c in range(NSIM) if topo.host(c) == topo.host(R) and topo.chip(c) == topo.chip(R) and c != R]
        able = [c for c in chip if all(topo.may_write(c, cores[j]) for j in row if j != i)]
        p0 = [c for c in able if topo.die(c) == topo.die(R)][0]
        p1 = [c for c in able if topo.die(c) != topo.die(R)][0]
        rm = [j for j in col if topo.rack(topo.host(cores[j])) == topo.rack(topo.host(R))][0]
        dg = [j for j in col if not topo.may_write(R, cores[j])][0]
        cb = [j for j in col if j not in (rm, dg)][0]
        info.append({"R": R, "row": row, "oth": [j for j in row if j != i], "P": (p0, p1), "rm": rm, "cb": cb, "dg": dg,
                     "host": topo.host(R), "place": row.index(i)})
        role[R] = ("R", i, 0)
        role[p0] = ("P", i, 0)
        role[p1] = ("P", i, 1)
    _PLAN["p"] = (info, role)
    return _PLAN["p"]


def _eng(topo, src, dst):
    return _bits(topo.mask(src, dst))


def _dst(topo, dst, src):
    rid, pid = topo.addr(dst, src)
    return DstId(rid=rid, pnc=pid)


def _rank_core(g, core, T, topo, info, i):
    d, S = info[i], T.sem
    al = _eng(topo, core, d["P"][0])
    lo = _eng(topo, core, info[d["rm"]]["P"][0])
    hi = [b for b in al if b not in lo]
    g.sync.dma_start(T.qsb[:, :], T.q[:, :]).then_inc(S.ldq, 16)
    g.scalar.dma_start(T.kv[:, D:3 * D], T.k[:, :]).then_inc(S.ldk, 16)
    g.sync.dma_start(T.kv[:, 0:D], T.v[:, 0:D]).then_inc(S.ldv0, 16)
    g.scalar.dma_start(T.kv[:, 3 * D:4 * D], T.v[:, D:2 * D]).then_inc(S.ldv1, 16)
    sent = 0
    g.wait_ge(S.ldq, 16)
    g.remote_dma_fused([
        RemoteDMATransfer(dst_ids=[_dst(topo, d["P"][x], core)], dma_engine_mask=_mk(hi[x::2]),
                          remote_sem=S.own, src=T.qsb[:, x * D:(x + 1) * D], dst=T.big[:, 0:D]) for x in (0, 1)],
        local_sem=S.snd)
    sent += len(hi)
    g.wait_ge(S.ldk, 16)
    g.wait_ge(S.ldv0, 16)
    g.wait_ge(S.ldv1, 16)
    slot = T.kvin[:, 2 * D * d["host"]:2 * D * (d["host"] + 1)]
    for n, pair in enumerate(((d["rm"], d["cb"]), (d["cb"], d["rm"]))):
        tr = []
        for x in (0, 1):
            to = info[pair[x]]["P"][x]
            par = 0 if pair[x] == d["rm"] else 1
            tr.append(RemoteDMATransfer(dst_ids=[_dst(topo, to, core)], dma_engine_mask=_mk(lo[par::2]),
                                        remote_sem=S["kvh%d" % d["host"]], src=T.kv[:, 2 * D * x:2 * D * (x + 1)], dst=slot))
            sent += len(lo[par::2])
            if n == 1:
                tr.append(RemoteDMATransfer(dst_ids=[_dst(topo, d["P"][x], core)], dma_engine_mask=_mk(hi[x::2]),
                                            remote_sem=S["kvh%d" % d["host"]], src=T.kv[:, 2 * D * x:2 * D * (x + 1)],
                                            dst=slot))
                sent += len(hi[x::2])
        g.remote_dma_fused(tr, local_sem=S.snd)
    oth = sorted(d["oth"], key=lambda j: 0 if topo.same_plane(core, info[j]["R"]) else 1)

    def got(j):
        if j == i:
            return sum(len(_eng(topo, d["P"][x], info[d["oth"][0]]["R"])) for x in (0, 1))
        return sum(len(_eng(topo, info[j]["P"][x], core)) // 2 for x in (0, 1))

    def blk(j):
        p = info[j]["place"]
        return T.part[:, 2 * D * p:2 * D * (p + 1)]

    v = g.vector
    v.wait_ge(S["pt%d" % d["place"]], got(i))
    v.tensor_copy(T.ps0[:, 0:2 * D], blk(i)).then_inc(S.a0, 1)
    v.wait_ge(S.a0, 1)
    v.wait_ge(S["pt%d" % info[oth[0]]["place"]], got(oth[0]))
    v.tensor_tensor(T.ps1[:, 0:2 * D], T.ps0[:, 0:2 * D], blk(oth[0]), AluOpType.add).then_inc(S.a1, 1)
    v.wait_ge(S.a1, 1)
    v.wait_ge(S["pt%d" % info[oth[1]]["place"]], got(oth[1]))
    v.tensor_tensor(T.ysb[:, :], T.ps1[:, 0:2 * D], blk(oth[1]), AluOpType.add).then_inc(S.a2, 1)
    g.sync.wait_ge(S.a2, 1)
    g.sync.dma_start(T.y[:, :], T.ysb[:, :]).then_inc(S.st, 16)
    g.sync.wait_ge(S.st, 16)
    g.wait_ge(S.snd, sent)


def _compute_core(g, core, T, topo, info, i, x):
    d, S = info[i], T.sem
    R = d["R"]
    first, second = (d["rm"], d["cb"]) if x == 0 else (d["cb"], d["rm"])
    onward = second
    off_r = _eng(topo, R, info[first]["P"][x])
    n_own = (len(_eng(topo, R, core)) - len(off_r)) // 2

    def kv_sem(j):
        return S["kvh%d" % info[j]["host"]]

    def kv_cols(j):
        return 2 * D * info[j]["host"]

    n_dir = {j: len(_eng(topo, info[j]["R"], core)) // 2 for j in (first, second)}
    n_fwd = len(_eng(topo, info[second]["P"][x], core))
    n_q = sum(len(_eng(topo, info[j]["P"][x], core)) for j in d["oth"])

    sent = 0
    g.wait_ge(S.own, n_own)
    lo = _eng(topo, core, info[d["oth"][0]]["P"][x])
    dsts = []
    for j in d["oth"]:
        s = 1 + info[j]["oth"].index(i)
        dsts.append(T.big[:, s * D:(1 + s) * D])
    g.remote_dma_fused([RemoteDMATransfer(dst_ids=[_dst(topo, info[j]["P"][x], core) for j in d["oth"]],
                                          dma_engine_mask=_mk(lo), remote_sem=S.qin,
                                          srcs=[T.big[:, 0:D]], dsts=dsts)], local_sem=S.snd)
    sent += len(lo)
    g.wait_ge(kv_sem(first), n_dir[first])
    to = info[onward]["P"][x]
    rid, pid = topo.addr(to, core)
    lo = _eng(topo, core, to)
    ap = T.kvin[:, kv_cols(first):kv_cols(first) + 2 * D]
    g.remote_dma(ap, ap, kv_sem(first), S.snd, pid, rid, _mk(lo))
    sent += len(lo)
    here = (2 * d["place"] + x) * D
    g.wait_ge(S.ca, 1)
    off = _eng(topo, core, info[d["oth"][0]]["R"])
    rid, pid = topo.addr(R, core)
    g.remote_dma(T.part[:, here:here + D], T.osb[:, 0:D], S["pt%d" % d["place"]], S.snd, pid, rid, _mk(off))
    sent += len(off)
    g.wait_ge(S.cb, 1)
    tr = []
    for k, j in enumerate(d["oth"]):
        lo = _eng(topo, core, info[j]["R"])
        hl = len(lo) // 2
        tr.append(RemoteDMATransfer(dst_ids=[_dst(topo, info[j]["R"], core)], dma_engine_mask=_mk(lo[k * hl:(k + 1) * hl]),
                                    remote_sem=S["pt%d" % d["place"]], src=T.osb[:, (1 + k) * D:(2 + k) * D],
                                    dst=T.part[:, here:here + D]))
        sent += hl
    g.remote_dma_fused(tr, local_sem=S.snd)
    g.wait_ge(S.snd, sent)

    ko, vo = (D, 0) if x == 0 else (0, D)
    blocks = (i, first, second, d["dg"])
    K = [T.kvin[:, kv_cols(j) + ko:kv_cols(j) + ko + D] for j in blocks]
    V = [T.kvin[:, kv_cols(j) + vo:kv_cols(j) + vo + D] for j in blocks]
    Q = {"a": T.big[:, 0:D], "b": T.big[:, D:3 * D]}
    W = {"a": D, "b": 2 * D}
    ACC = {"a": T.psa[:, 0:D], "b": T.psb[:, 0:2 * D]}
    DONE = {"a": S.oa, "b": S.ob}
    offs, o = [], 0
    for (_, grp) in TILES:
        offs.append(o)
        o += W[grp]
    arrive = [(kv_sem(i), n_own), (kv_sem(first), n_dir[first]), (kv_sem(second), n_dir[second]), (kv_sem(d["dg"]), n_fwd)]

    te = g.tensor
    seen = {"k": set(), "q": False, "o": False}

    def s_mm(t):
        j, grp = TILES[t]
        if not seen["o"]:
            te.wait_ge(S.own, n_own)
            seen["o"] = True
        if j not in seen["k"]:
            te.wait_ge(arrive[j][0], arrive[j][1])
            seen["k"].add(j)
        if grp == "b" and not seen["q"]:
            te.wait_ge(S.qin, n_q)
            seen["q"] = True
        te.matmul(T["ps%d" % (t % NSB)][:, 0:W[grp]], K[j], Q[grp], True, True).then_inc(S["m%d" % t], 1)

    def o_mm(t):
        j, grp = TILES[t]
        same = [u for u in range(len(TILES)) if TILES[u][1] == grp]
        te.wait_ge(S["r%d" % t], 1)
        mm = te.matmul(ACC[grp], V[j], T.ssb[:, offs[t]:offs[t] + W[grp]], t == same[0], t == same[-1])
        if t == same[-1]:
            mm.then_inc(DONE[grp], 1)

    for kind, t in (("s", 0), ("s", 1), ("o", 0), ("s", 2), ("o", 1), ("s", 3), ("o", 2), ("s", 4), ("o", 3), ("s", 5),
                    ("o", 4), ("o", 5), ("s", 6), ("s", 7), ("o", 6), ("o", 7)):
        if kind == "s":
            s_mm(t)
        else:
            o_mm(t)

    v = g.vector
    v.memset(T.zeros[:, :], 0.0).then_inc(S.zs, 1)
    v.wait_ge(S.zs, 1)
    for t, (_, grp) in enumerate(TILES):
        v.wait_ge(S["m%d" % t], 1)
        v.tensor_tensor(T.ssb[:, offs[t]:offs[t] + W[grp]], T["ps%d" % (t % NSB)][:, 0:W[grp]], T.zeros[:, 0:W[grp]],
                        AluOpType.max).then_inc(S["r%d" % t], 1)
    v.wait_ge(S.oa, 1)
    v.tensor_copy(T.osb[:, 0:D], T.psa[:, 0:D]).then_inc(S.ca, 1)
    v.wait_ge(S.ob, 1)
    v.tensor_copy(T.osb[:, D:3 * D], T.psb[:, 0:2 * D]).then_inc(S.cb, 1)


def rank_program(g, core, T, topo):
    info, role = _plan(T, topo)
    if core not in role:
        return
    kind, i, x = role[core]
    if kind == "R":
        _rank_core(g, core, T, topo, info, i)
    else:
        _compute_core(g, core, T, topo, info, i, x)
